import numpy as np
import ml_dtypes


def mxq(x, axis, fmt="e4m3"):
    dtype, down = {"e4m3": (ml_dtypes.float8_e4m3fn, 7), "e5m2": (ml_dtypes.float8_e5m2, 14)}[fmt]
    v = np.moveaxis(np.asarray(x, np.float32).astype(ml_dtypes.bfloat16).astype(np.float64), axis, -1)
    blocks = v.reshape(v.shape[:-1] + (-1, 32))
    amax = np.abs(blocks).max(-1, keepdims=True)
    byte = np.maximum(np.where(amax > 0, np.frexp(amax)[1] - 1 + 127, 0) - down, 1)
    scale = np.exp2(byte - 127.0)
    codes = (blocks / scale).astype(np.float32).astype(dtype).astype(np.float64)
    return np.moveaxis((codes * scale).reshape(v.shape), -1, axis)


WIDE = False


def mx_kscale(k):
    if not WIDE:
        return np.ones(k)
    levels = np.array([10, -10, 5, -5, 0])
    if k % 512:
        return np.exp2(np.random.permutation(np.resize(levels, k // 32))).repeat(32)
    a = np.empty((k // 512, 16))
    for p in range(k // 512):
        a[p, :8] = np.random.permutation(np.resize(levels, 8))
        for g in range(8):
            far = levels[np.abs(levels - a[p, g]) >= 10]
            a[p, g + 8] = far[np.random.randint(len(far))]
    return np.exp2(a.ravel()).repeat(32)


def f64(x):
    return np.asarray(x).astype(np.float64)


def striped8(idx):
    return np.asarray(idx).reshape(8, -1, 16).transpose(0, 2, 1).reshape(128, -1).astype(np.uint16)


def unstriped8(offs):
    return offs.reshape(8, 16, -1).transpose(0, 2, 1).reshape(8, -1).astype(np.int64)


def pick8(x, idx, run):
    r = np.arange(len(x))
    return x[r[:, None], idx[r % (8 * run) // run]]


E2M1 = np.array([0.0, 0.5, 1.0, 1.5, 2.0, 3.0, 4.0, 6.0, -0.0, -0.5, -1.0, -1.5, -2.0, -3.0, -4.0, -6.0])


def pack_weight(w, fmt):
    k, n = w.shape
    w = f64(np.asarray(w, np.float32).astype(ml_dtypes.bfloat16)).reshape(k // 32, 32, n)
    amax = np.abs(w).max(1)
    if fmt == "e4m3":
        byte = np.frexp(amax)[1] - 1 + 127 - 7
    else:
        mant, ex = np.frexp(amax / 6.0)
        byte = np.where(mant > 0.5, ex, ex - 1) + 127
    byte = np.clip(np.where(amax > 0, byte, 1), 1, 254)
    scaled = (w * np.exp2(127.0 - byte)[:, None, :]).reshape(k, n).astype(np.float32)
    by_word = np.ascontiguousarray(scaled.reshape(k // 512, 128, 4, n).transpose(0, 1, 3, 2))
    if fmt == "e4m3":
        words = by_word.astype(ml_dtypes.float8_e4m3fn).view(np.uint8)
    else:
        c = by_word.astype(ml_dtypes.float4_e2m1fn).view(np.uint8) & 0xF
        words = (c[..., 0::2] | (c[..., 1::2] << 4)).reshape(k // 512, 128, 2 * n)
    return np.ascontiguousarray(words), np.ascontiguousarray(byte.astype(np.uint8).reshape(k // 512, 16, n))


def unpack_weight(words, scales, fmt):
    g, _, n = scales.shape
    words = np.ascontiguousarray(words).reshape(g, 128, n, -1)
    if fmt == "e4m3":
        vals = words.view(ml_dtypes.float8_e4m3fn).astype(np.float64)
    else:
        nib = np.empty((g, 128, n, 4), np.uint8)
        nib[..., 0::2] = words & 0xF
        nib[..., 1::2] = words >> 4
        vals = E2M1[nib]
    vals = vals * np.repeat(np.exp2(scales.astype(np.float64) - 127.0), 8, axis=1)[..., None]
    return vals.transpose(0, 1, 3, 2).reshape(g * 512, n)


D, T, U, X, S, I, Q = 512, 1024, 1024, 1024, 1024, 512, 128


def setup_inputs():
    n = np.random.standard_normal
    idx = np.stack([np.random.permutation(T)[:I] for _ in range(8)])
    idx2 = np.stack([np.random.permutation(U)[:I] for _ in range(8)])
    idx3 = np.stack([np.random.permutation(X)[:I] for _ in range(8)])
    idx4 = np.stack([np.random.permutation(S)[:I] for _ in range(8)])
    idx5 = np.stack([np.random.permutation(X)[:I] for _ in range(8)])
    idx6 = np.stack([np.random.permutation(S)[:I] for _ in range(8)])
    fd = mx_kscale(D)
    keysp = pack_weight(n((D, T)) / fd[:, None], "e2m1")
    notesp = pack_weight(n((D, U)) / fd[:, None], "e4m3")
    usersp = pack_weight(n((D, X)) / fd[:, None], "e2m1")
    shelvesp = pack_weight(n((D, S)) / fd[:, None], "e4m3")
    return {
        "query": (n((D, Q)) * 1.0 / np.sqrt(D) * fd[:, None]).astype(np.float32),
        "keys_words": keysp[0],
        "keys_scales": keysp[1],
        "notes_words": notesp[0],
        "notes_scales": notesp[1],
        "users_words": usersp[0],
        "users_scales": usersp[1],
        "shelves_words": shelvesp[0],
        "shelves_scales": shelvesp[1],
        "offs": striped8(idx),
        "offs2": striped8(idx2),
        "offs3": striped8(idx3),
        "offs4": striped8(idx4),
        "offs5": striped8(idx5),
        "offs6": striped8(idx6),
    }


def reference(query, keys_words, keys_scales, notes_words, notes_scales, users_words, users_scales, shelves_words, shelves_scales, offs, offs2, offs3, offs4, offs5, offs6):
    idx = unstriped8(offs)
    idx2 = unstriped8(offs2)
    idx3 = unstriped8(offs3)
    idx4 = unstriped8(offs4)
    idx5 = unstriped8(offs5)
    idx6 = unstriped8(offs6)
    keysu = unpack_weight(keys_words, keys_scales, "e2m1")
    notesu = unpack_weight(notes_words, notes_scales, "e4m3")
    usersu = unpack_weight(users_words, users_scales, "e2m1")
    shelvesu = unpack_weight(shelves_words, shelves_scales, "e4m3")
    queryq = mxq(f64(query), 0, "e4m3")
    a = queryq.T @ keysu
    b = queryq.T @ notesu
    c0 = queryq.T @ usersu
    d0 = queryq.T @ shelvesu
    r = pick8(a, idx, 16) - pick8(b, idx2, 16)
    f1 = np.zeros((Q, X))
    f1[np.arange(Q)[:, None], idx3[np.arange(Q) % 128 // 16]] = r
    f2 = np.zeros((Q, S))
    f2[np.arange(Q)[:, None], idx4[np.arange(Q) % 128 // 16]] = r
    cc = c0 + f1
    dd = d0 - f2
    y = pick8(cc, idx5, 16) - pick8(dd, idx6, 16)
    return y

@@ -1,0 +1,168 @@
+from contextlib import ExitStack
+
+import concourse.mybir as mybir
+
+F32 = mybir.dt.float32
+BF16 = mybir.dt.bfloat16
+I32 = mybir.dt.int32
+U32 = mybir.dt.uint32
+U16 = mybir.dt.uint16
+U8 = mybir.dt.uint8
+FP8X4 = mybir.dt.float8_e4m3fn_x4
+FP4X4 = mybir.dt.float4_e2m1fn_x4
+ADD = mybir.AluOpType.add
+SUB = mybir.AluOpType.subtract
+COPY = mybir.ActivationFunctionType.Copy
+
+P = 128
+PACK = 4
+POOL = 1024
+SLOTS = 512
+HALF = SLOTS // 2
+BANK = 512
+FLOPS = 2 * 512 * 128 * 4 * POOL
+
+
+def tile_attend_audit_four_kernel(
+    tc, query, keys_words, keys_scales, notes_words, notes_scales, users_words, users_scales,
+    shelves_words, shelves_scales, offs, offs2, offs3, offs4, offs5, offs6, out,
+):
+    nc = tc.nc
+    with ExitStack() as ctx:
+        lists = ctx.enter_context(tc.tile_pool(name="lists", bufs=1))
+        sb = ctx.enter_context(tc.tile_pool(name="sb", bufs=1))
+        psum = ctx.enter_context(tc.psum_pool(name="psum", bufs=1))
+
+        def scale_tile(name):
+            plane = sb.tile([P, POOL], U8, name=name, align_bytes=64)
+            nc.vector.memset(plane[:].bitcast(I32), 0)
+            return plane
+
+        def load_scale_rows(queue, plane, scales, quad):
+            queue.dma_start(
+                out=plane[32 * quad : 32 * quad + 4, :].bitcast(I32),
+                in_=scales[0, 4 * quad : 4 * quad + 4, :].bitcast(I32),
+            )
+
+        def load_fp4(name, words):
+            codes = sb.tile([P, 2 * POOL], U8, name=name, align_bytes=64)
+            nc.sync.dma_start(out=codes[:].bitcast(I32), in_=words[0].bitcast(I32))
+            return codes
+
+        def load_fp8(name, words):
+            codes = sb.tile([P, POOL], U32, name=name, align_bytes=64)
+            nc.sync.dma_start(
+                out=codes[:].bitcast(I32), in_=words[0].rearrange("p n t -> p (n t)").bitcast(I32)
+            )
+            return codes
+
+        def load_list(name, src):
+            tile = lists.tile([P, SLOTS // 16], U16, name=name)
+            nc.sync.dma_start(tile[:], src)
+            return tile
+
+        notes_plane = scale_tile("notes_plane")
+        keys_plane = scale_tile("keys_plane")
+        shelves_plane = scale_tile("shelves_plane")
+        users_plane = scale_tile("users_plane")
+        f1 = sb.tile([P, POOL], F32, name="f1")
+        f2 = sb.tile([P, POOL], F32, name="f2")
+        nc.vector.memset(f2[:], 0.0)
+        nc.vector.memset(f1[:], 0.0)
+
+        q_raw = sb.tile([P, PACK, P], F32, name="q_raw")
+        nc.sync.dma_start(out=q_raw[:], in_=query.rearrange("(p j) w -> p j w", j=PACK))
+        for quad in range(4):
+            load_scale_rows(nc.scalar, notes_plane, notes_scales, quad)
+        load_scale_rows(nc.sync, keys_plane, keys_scales, 0)
+        notes_codes = load_fp8("notes_codes", notes_words)
+        keys_codes = load_fp4("keys_codes", keys_words)
+        for quad in range(1, 4):
+            load_scale_rows(nc.sync, keys_plane, keys_scales, quad)
+        note_list = load_list("note_list", offs2)
+        token_list = load_list("token_list", offs)
+        shelf_put_list = load_list("shelf_put_list", offs4)
+        shelves_codes = load_fp8("shelves_codes", shelves_words)
+        for quad in range(4):
+            load_scale_rows(nc.sync, shelves_plane, shelves_scales, quad)
+        user_put_list = load_list("user_put_list", offs3)
+        shelf_get_list = load_list("shelf_get_list", offs6)
+        users_codes = load_fp4("users_codes", users_words)
+        for quad in range(4):
+            load_scale_rows(nc.sync, users_plane, users_scales, quad)
+        user_get_list = load_list("user_get_list", offs5)
+
+        q_bf = sb.tile([P, P, PACK], BF16, name="q_bf", align_bytes=64)
+        nc.vector.tensor_copy(out=q_bf[:], in_=q_raw[:].rearrange("p j w -> p w j"))
+        q_codes = sb.tile([P, P], U32, name="q_codes", align_bytes=64)
+        q_plane = sb.tile([P, P], U8, name="q_plane", align_bytes=64)
+        nc.vector.quantize_mx(
+            out=q_codes[:].bitcast(FP8X4), scales=q_plane[:], in_=q_bf[:].rearrange("p w j -> p (w j)")
+        )
+
+        def score(bank, codes, plane, col0, width, is_fp4):
+            if is_fp4:
+                moving = codes[:, 2 * col0 : 2 * (col0 + width)].bitcast(FP4X4)
+            else:
+                moving = codes[:, col0 : col0 + width].bitcast(FP8X4)
+            nc.tensor.matmul_mx(
+                out=bank[:, 0:width], lhsT=q_codes[:].bitcast(FP8X4), lhsT_scale=q_plane[:],
+                rhs=moving, rhs_scale=plane[:, col0 : col0 + width], start=True, stop=True,
+            )
+
+        banks = [psum.tile([P, BANK], F32, name="bank%d" % n) for n in range(8)]
+
+        def half_list(tile, h):
+            return tile[:, h * (HALF // 16) : (h + 1) * (HALF // 16)]
+
+        def half(tile, h):
+            return tile[:, h * HALF : (h + 1) * HALF]
+
+        b = sb.tile([P, POOL], F32, name="b")
+        score(banks[0], notes_codes, notes_plane, 0, BANK, False)
+        score(banks[1], notes_codes, notes_plane, BANK, BANK, False)
+        nc.vector.tensor_copy(out=b[:, 0:BANK], in_=banks[0][:])
+        nc.scalar.activation(b[:, BANK:POOL], banks[1][:], COPY)
+
+        a = sb.tile([P, POOL], F32, name="a")
+        quarter = POOL // 4
+        for n in range(4):
+            score(banks[2 + n], keys_codes, keys_plane, n * quarter, quarter, True)
+            nc.vector.tensor_copy(out=a[:, n * quarter : (n + 1) * quarter], in_=banks[2 + n][:, 0:quarter])
+
+        b_got = sb.tile([P, SLOTS], F32, name="b_got")
+        for h in range(2):
+            nc.scalar.activation(half(b_got, h), b[:].indirect(half_list(note_list, h)), COPY)
+
+        r = sb.tile([P, SLOTS], F32, name="r")
+        nc.vector.tensor_tensor(half(r, 0), a[:].indirect(half_list(token_list, 0)), half(b_got, 0), SUB)
+        a_got = sb.tile([P, HALF], F32, name="a_got")
+        nc.scalar.activation(a_got[:], a[:].indirect(half_list(token_list, 1)), COPY)
+        nc.gpsimd.tensor_tensor(half(r, 1), a_got[:], half(b_got, 1), SUB)
+
+        for h in range(2):
+            nc.vector.tensor_copy(f2[:].indirect(half_list(shelf_put_list, h)), half(r, h))
+        nc.vector.tensor_copy(f1[:].indirect(user_put_list[:]), r[:])
+
+        d0 = sb.tile([P, POOL], F32, name="d0")
+        for n in range(2):
+            score(banks[6 + n], shelves_codes, shelves_plane, n * BANK, BANK, False)
+            nc.scalar.activation(d0[:, n * BANK : (n + 1) * BANK], banks[6 + n][:], COPY)
+        dd = sb.tile([P, POOL], F32, name="dd")
+        nc.gpsimd.tensor_tensor(dd[:], d0[:], f2[:], SUB)
+        dd_got = sb.tile([P, SLOTS], F32, name="dd_got")
+        nc.scalar.activation(dd_got[:], dd[:].indirect(shelf_get_list[:]), COPY)
+
+        cc = sb.tile([P, POOL], F32, name="cc")
+        for n in range(2):
+            score(banks[n], users_codes, users_plane, n * BANK, BANK, True)
+            cols = slice(n * BANK, (n + 1) * BANK)
+            nc.vector.tensor_tensor(cc[:, cols], banks[n][:], f1[:, cols], ADD)
+
+        y = sb.tile([P, SLOTS], F32, name="y")
+        nc.vector.tensor_tensor(half(y, 0), cc[:].indirect(half_list(user_get_list, 0)), half(dd_got, 0), SUB)
+        nc.sync.dma_start(out=out[:, 0:HALF], in_=half(y, 0))
+        cc_got = sb.tile([P, HALF], F32, name="cc_got")
+        nc.scalar.activation(cc_got[:], cc[:].indirect(half_list(user_get_list, 1)), COPY)
+        nc.vector.tensor_tensor(half(y, 1), cc_got[:], half(dd_got, 1), SUB)
+        nc.sync.dma_start(out=out[:, HALF:SLOTS], in_=half(y, 1))

@@ -20,6 +20,7 @@ POOL = 1024
 SLOTS = 512
 HALF = SLOTS // 2
 BANK = 512
+GP_COLS = 256
 FLOPS = 2 * 512 * 128 * 4 * POOL
 
 
@@ -49,11 +50,10 @@ def tile_attend_audit_four_kernel(
             nc.sync.dma_start(out=codes[:].bitcast(I32), in_=words[0].bitcast(I32))
             return codes
 
-        def load_fp8(name, words):
-            codes = sb.tile([P, POOL], U32, name=name, align_bytes=64)
-            nc.sync.dma_start(
-                out=codes[:].bitcast(I32), in_=words[0].rearrange("p n t -> p (n t)").bitcast(I32)
-            )
+        def load_fp8(name, words, col0, width):
+            codes = sb.tile([P, width], U32, name=name, align_bytes=64)
+            src = words[0].rearrange("p n t -> p (n t)")[:, PACK * col0 : PACK * (col0 + width)]
+            nc.sync.dma_start(out=codes[:].bitcast(I32), in_=src.bitcast(I32))
             return codes
 
         def load_list(name, src):
@@ -63,52 +63,57 @@ def tile_attend_audit_four_kernel(
 
         notes_plane = scale_tile("notes_plane")
         keys_plane = scale_tile("keys_plane")
-        shelves_plane = scale_tile("shelves_plane")
         users_plane = scale_tile("users_plane")
-        f1 = sb.tile([P, POOL], F32, name="f1")
+        shelves_plane = scale_tile("shelves_plane")
         f2 = sb.tile([P, POOL], F32, name="f2")
         nc.vector.memset(f2[:], 0.0)
-        nc.vector.memset(f1[:], 0.0)
 
         q_raw = sb.tile([P, PACK, P], F32, name="q_raw")
         nc.sync.dma_start(out=q_raw[:], in_=query.rearrange("(p j) w -> p j w", j=PACK))
         for quad in range(4):
-            load_scale_rows(nc.scalar, notes_plane, notes_scales, quad)
-        load_scale_rows(nc.sync, keys_plane, keys_scales, 0)
-        notes_codes = load_fp8("notes_codes", notes_words)
+            load_scale_rows(nc.sync, notes_plane, notes_scales, quad)
+        notes_codes = [load_fp8("notes_codes%d" % h, notes_words, h * BANK, BANK) for h in range(2)]
         keys_codes = load_fp4("keys_codes", keys_words)
-        for quad in range(1, 4):
+        for quad in range(4):
             load_scale_rows(nc.sync, keys_plane, keys_scales, quad)
         note_list = load_list("note_list", offs2)
         token_list = load_list("token_list", offs)
         shelf_put_list = load_list("shelf_put_list", offs4)
-        shelves_codes = load_fp8("shelves_codes", shelves_words)
+        users_codes = load_fp4("users_codes", users_words)
+        for quad in range(4):
+            load_scale_rows(nc.sync, users_plane, users_scales, quad)
+        shelves_codes = load_fp8("shelves_codes", shelves_words, 0, POOL)
         for quad in range(4):
             load_scale_rows(nc.sync, shelves_plane, shelves_scales, quad)
         user_put_list = load_list("user_put_list", offs3)
         shelf_get_list = load_list("shelf_get_list", offs6)
-        users_codes = load_fp4("users_codes", users_words)
-        for quad in range(4):
-            load_scale_rows(nc.sync, users_plane, users_scales, quad)
         user_get_list = load_list("user_get_list", offs5)
 
-        q_bf = sb.tile([P, P, PACK], BF16, name="q_bf", align_bytes=64)
-        nc.vector.tensor_copy(out=q_bf[:], in_=q_raw[:].rearrange("p j w -> p w j"))
+        q_bf = sb.tile([P, P, PACK], BF16, name="q_bf", tag="q_bf_then_f1", align_bytes=64)
         q_codes = sb.tile([P, P], U32, name="q_codes", align_bytes=64)
         q_plane = sb.tile([P, P], U8, name="q_plane", align_bytes=64)
-        nc.vector.quantize_mx(
-            out=q_codes[:].bitcast(FP8X4), scales=q_plane[:], in_=q_bf[:].rearrange("p w j -> p (w j)")
-        )
-
-        def score(bank, codes, plane, col0, width, is_fp4):
-            if is_fp4:
-                moving = codes[:, 2 * col0 : 2 * (col0 + width)].bitcast(FP4X4)
-            else:
-                moving = codes[:, col0 : col0 + width].bitcast(FP8X4)
-            nc.tensor.matmul_mx(
-                out=bank[:, 0:width], lhsT=q_codes[:].bitcast(FP8X4), lhsT_scale=q_plane[:],
-                rhs=moving, rhs_scale=plane[:, col0 : col0 + width], start=True, stop=True,
+        row_halves = [slice(0, P // 2), slice(P // 2, P)]
+        for rows in row_halves:
+            nc.vector.tensor_copy(out=q_bf[:, rows, :], in_=q_raw[:, :, rows].rearrange("p j w -> p w j"))
+        for rows in row_halves:
+            nc.vector.quantize_mx(
+                out=q_codes[:, rows].bitcast(FP8X4), scales=q_plane[:, rows],
+                in_=q_bf[:, rows, :].rearrange("p w j -> p (w j)"),
             )
+        f1 = sb.tile([P, POOL], F32, name="f1", tag="q_bf_then_f1", align_bytes=64)
+        nc.gpsimd.memset(f1[:], 0.0)
+
+        def score(dst, moving, moving_scale):
+            nc.tensor.matmul_mx(
+                out=dst, lhsT=q_codes[:].bitcast(FP8X4), lhsT_scale=q_plane[:],
+                rhs=moving, rhs_scale=moving_scale, start=True, stop=True,
+            )
+
+        def fp4_cols(codes, col0, width):
+            return codes[:, 2 * col0 : 2 * (col0 + width)].bitcast(FP4X4)
+
+        def fp8_cols(codes, col0, width):
+            return codes[:, col0 : col0 + width].bitcast(FP8X4)
 
         banks = [psum.tile([P, BANK], F32, name="bank%d" % n) for n in range(8)]
 
@@ -118,17 +123,23 @@ def tile_attend_audit_four_kernel(
         def half(tile, h):
             return tile[:, h * HALF : (h + 1) * HALF]
 
+        quarter = POOL // 4
         b = sb.tile([P, POOL], F32, name="b")
-        score(banks[0], notes_codes, notes_plane, 0, BANK, False)
-        score(banks[1], notes_codes, notes_plane, BANK, BANK, False)
-        nc.vector.tensor_copy(out=b[:, 0:BANK], in_=banks[0][:])
-        nc.scalar.activation(b[:, BANK:POOL], banks[1][:], COPY)
+        for n in range(4):
+            cols = slice(n * quarter, (n + 1) * quarter)
+            src = banks[n][:, 0:quarter]
+            score(src, fp8_cols(notes_codes[n // 2], (n % 2) * quarter, quarter), notes_plane[:, cols])
+            if n % 2 == 0:
+                nc.scalar.activation(b[:, cols], src, COPY)
+            else:
+                nc.vector.tensor_copy(out=b[:, cols], in_=src)
 
         a = sb.tile([P, POOL], F32, name="a")
-        quarter = POOL // 4
         for n in range(4):
-            score(banks[2 + n], keys_codes, keys_plane, n * quarter, quarter, True)
-            nc.vector.tensor_copy(out=a[:, n * quarter : (n + 1) * quarter], in_=banks[2 + n][:, 0:quarter])
+            cols = slice(n * quarter, (n + 1) * quarter)
+            src = banks[4 + n][:, 0:quarter]
+            score(src, fp4_cols(keys_codes, n * quarter, quarter), keys_plane[:, cols])
+            nc.vector.tensor_copy(out=a[:, cols], in_=src)
 
         b_got = sb.tile([P, SLOTS], F32, name="b_got")
         for h in range(2):
@@ -144,20 +155,28 @@ def tile_attend_audit_four_kernel(
             nc.vector.tensor_copy(f2[:].indirect(half_list(shelf_put_list, h)), half(r, h))
         nc.vector.tensor_copy(f1[:].indirect(user_put_list[:]), r[:])
 
+        split = POOL - GP_COLS
+        c0_tail = sb.tile([P, GP_COLS], F32, name="c0_tail")
+        score(banks[0][:, 0:GP_COLS], fp4_cols(users_codes, split, GP_COLS), users_plane[:, split:POOL])
+        nc.scalar.activation(c0_tail[:], banks[0][:, 0:GP_COLS], COPY)
+        score(banks[2][:], fp4_cols(users_codes, 0, BANK), users_plane[:, 0:BANK])
+        score(banks[3][:, 0 : split - BANK], fp4_cols(users_codes, BANK, split - BANK), users_plane[:, BANK:split])
+
         d0 = sb.tile([P, POOL], F32, name="d0")
-        for n in range(2):
-            score(banks[6 + n], shelves_codes, shelves_plane, n * BANK, BANK, False)
-            nc.scalar.activation(d0[:, n * BANK : (n + 1) * BANK], banks[6 + n][:], COPY)
+        for n in (1, 0):
+            cols = slice(n * BANK, (n + 1) * BANK)
+            score(banks[n][:], fp8_cols(shelves_codes, n * BANK, BANK), shelves_plane[:, cols])
+            nc.scalar.activation(d0[:, cols], banks[n][:], COPY)
+
         dd = sb.tile([P, POOL], F32, name="dd")
         nc.gpsimd.tensor_tensor(dd[:], d0[:], f2[:], SUB)
         dd_got = sb.tile([P, SLOTS], F32, name="dd_got")
         nc.scalar.activation(dd_got[:], dd[:].indirect(shelf_get_list[:]), COPY)
 
         cc = sb.tile([P, POOL], F32, name="cc")
-        for n in range(2):
-            score(banks[n], users_codes, users_plane, n * BANK, BANK, True)
-            cols = slice(n * BANK, (n + 1) * BANK)
-            nc.vector.tensor_tensor(cc[:, cols], banks[n][:], f1[:, cols], ADD)
+        nc.gpsimd.tensor_tensor(cc[:, split:POOL], c0_tail[:], f1[:, split:POOL], ADD)
+        nc.vector.tensor_tensor(cc[:, 0:BANK], banks[2][:], f1[:, 0:BANK], ADD)
+        nc.vector.tensor_tensor(cc[:, BANK:split], banks[3][:, 0 : split - BANK], f1[:, BANK:split], ADD)
 
         y = sb.tile([P, SLOTS], F32, name="y")
         nc.vector.tensor_tensor(half(y, 0), cc[:].indirect(half_list(user_get_list, 0)), half(dd_got, 0), SUB)

@@ -93,8 +93,9 @@ def tile_attend_audit_four_kernel(
         q_codes = sb.tile([P, P], U32, name="q_codes", align_bytes=64)
         q_plane = sb.tile([P, P], U8, name="q_plane", align_bytes=64)
         row_halves = [slice(0, P // 2), slice(P // 2, P)]
-        for rows in row_halves:
-            nc.vector.tensor_copy(out=q_bf[:, rows, :], in_=q_raw[:, :, rows].rearrange("p j w -> p w j"))
+        lo, hi = row_halves
+        nc.vector.tensor_copy(out=q_bf[:, lo, :], in_=q_raw[:, :, lo].rearrange("p j w -> p w j"))
+        nc.scalar.activation(q_bf[:, hi, :], q_raw[:, :, hi].rearrange("p j w -> p w j"), COPY)
         for rows in row_halves:
             nc.vector.quantize_mx(
                 out=q_codes[:, rows].bitcast(FP8X4), scales=q_plane[:, rows],
@@ -135,11 +136,13 @@ def tile_attend_audit_four_kernel(
                 nc.vector.tensor_copy(out=b[:, cols], in_=src)
 
         a = sb.tile([P, POOL], F32, name="a")
-        for n in range(4):
-            cols = slice(n * quarter, (n + 1) * quarter)
-            src = banks[4 + n][:, 0:quarter]
-            score(src, fp4_cols(keys_codes, n * quarter, quarter), keys_plane[:, cols])
+        col0 = 0
+        for bank, width in zip((4, 5, 6, 7, 0), (256, 256, 256, 128, 128)):
+            cols = slice(col0, col0 + width)
+            src = banks[bank][:, 0:width]
+            score(src, fp4_cols(keys_codes, col0, width), keys_plane[:, cols])
             nc.vector.tensor_copy(out=a[:, cols], in_=src)
+            col0 = col0 + width
 
         b_got = sb.tile([P, SLOTS], F32, name="b_got")
         for h in range(2):
@@ -162,7 +165,7 @@ def tile_attend_audit_four_kernel(
         score(banks[2][:], fp4_cols(users_codes, 0, BANK), users_plane[:, 0:BANK])
         score(banks[3][:, 0 : split - BANK], fp4_cols(users_codes, BANK, split - BANK), users_plane[:, BANK:split])
 
-        d0 = sb.tile([P, POOL], F32, name="d0")
+        d0 = sb.tile([P, POOL], F32, name="d0", tag="d0_then_cc")
         for n in (1, 0):
             cols = slice(n * BANK, (n + 1) * BANK)
             score(banks[n][:], fp8_cols(shelves_codes, n * BANK, BANK), shelves_plane[:, cols])
@@ -171,9 +174,10 @@ def tile_attend_audit_four_kernel(
         dd = sb.tile([P, POOL], F32, name="dd")
         nc.gpsimd.tensor_tensor(dd[:], d0[:], f2[:], SUB)
         dd_got = sb.tile([P, SLOTS], F32, name="dd_got")
-        nc.scalar.activation(dd_got[:], dd[:].indirect(shelf_get_list[:]), COPY)
+        for h in range(2):
+            nc.scalar.activation(half(dd_got, h), dd[:].indirect(half_list(shelf_get_list, h)), COPY)
 
-        cc = sb.tile([P, POOL], F32, name="cc")
+        cc = sb.tile([P, POOL], F32, name="cc", tag="d0_then_cc")
         nc.gpsimd.tensor_tensor(cc[:, split:POOL], c0_tail[:], f1[:, split:POOL], ADD)
         nc.vector.tensor_tensor(cc[:, 0:BANK], banks[2][:], f1[:, 0:BANK], ADD)
         nc.vector.tensor_tensor(cc[:, BANK:split], banks[3][:, 0 : split - BANK], f1[:, BANK:split], ADD)

@@ -51,7 +51,7 @@ def tile_attend_audit_four_kernel(
             return codes
 
         def load_fp8(name, words, col0, width):
-            codes = sb.tile([P, width], U32, name=name, align_bytes=64)
+            codes = sb.tile([P, width], U32, name=name, tag=name, align_bytes=64)
             src = words[0].rearrange("p n t -> p (n t)")[:, PACK * col0 : PACK * (col0 + width)]
             nc.sync.dma_start(out=codes[:].bitcast(I32), in_=src.bitcast(I32))
             return codes
@@ -63,46 +63,45 @@ def tile_attend_audit_four_kernel(
 
         notes_plane = scale_tile("notes_plane")
         keys_plane = scale_tile("keys_plane")
-        users_plane = scale_tile("users_plane")
         shelves_plane = scale_tile("shelves_plane")
-        f2 = sb.tile([P, POOL], F32, name="f2")
-        nc.vector.memset(f2[:], 0.0)
+        users_plane = scale_tile("users_plane")
+        f2_lo = sb.tile([P, POOL], F32, name="f2_lo")
+        nc.vector.memset(f2_lo[:], 0.0)
 
         q_raw = sb.tile([P, PACK, P], F32, name="q_raw")
         nc.sync.dma_start(out=q_raw[:], in_=query.rearrange("(p j) w -> p j w", j=PACK))
         for quad in range(4):
-            load_scale_rows(nc.sync, notes_plane, notes_scales, quad)
+            load_scale_rows(nc.sync if quad < 2 else nc.scalar, notes_plane, notes_scales, quad)
         notes_codes = [load_fp8("notes_codes%d" % h, notes_words, h * BANK, BANK) for h in range(2)]
         keys_codes = load_fp4("keys_codes", keys_words)
         for quad in range(4):
             load_scale_rows(nc.sync, keys_plane, keys_scales, quad)
         note_list = load_list("note_list", offs2)
+        shelves_codes = load_fp8("shelves_codes", shelves_words, 0, POOL)
         token_list = load_list("token_list", offs)
         shelf_put_list = load_list("shelf_put_list", offs4)
+        for quad in range(4):
+            load_scale_rows(nc.sync, shelves_plane, shelves_scales, quad)
         users_codes = load_fp4("users_codes", users_words)
         for quad in range(4):
             load_scale_rows(nc.sync, users_plane, users_scales, quad)
-        shelves_codes = load_fp8("shelves_codes", shelves_words, 0, POOL)
-        for quad in range(4):
-            load_scale_rows(nc.sync, shelves_plane, shelves_scales, quad)
         user_put_list = load_list("user_put_list", offs3)
         shelf_get_list = load_list("shelf_get_list", offs6)
         user_get_list = load_list("user_get_list", offs5)
 
-        q_bf = sb.tile([P, P, PACK], BF16, name="q_bf", tag="q_bf_then_f1", align_bytes=64)
         q_codes = sb.tile([P, P], U32, name="q_codes", align_bytes=64)
         q_plane = sb.tile([P, P], U8, name="q_plane", align_bytes=64)
-        row_halves = [slice(0, P // 2), slice(P // 2, P)]
-        lo, hi = row_halves
+        lo, hi = slice(0, P // 2), slice(P // 2, P)
+        q_bf = sb.tile([P, P, PACK], BF16, name="q_bf", tag="q_bf_then_f2", align_bytes=64)
         nc.vector.tensor_copy(out=q_bf[:, lo, :], in_=q_raw[:, :, lo].rearrange("p j w -> p w j"))
         nc.scalar.activation(q_bf[:, hi, :], q_raw[:, :, hi].rearrange("p j w -> p w j"), COPY)
-        for rows in row_halves:
+        for rows in (lo, hi):
             nc.vector.quantize_mx(
                 out=q_codes[:, rows].bitcast(FP8X4), scales=q_plane[:, rows],
                 in_=q_bf[:, rows, :].rearrange("p w j -> p (w j)"),
             )
-        f1 = sb.tile([P, POOL], F32, name="f1", tag="q_bf_then_f1", align_bytes=64)
-        nc.gpsimd.memset(f1[:], 0.0)
+        f2_hi = sb.tile([P, POOL], F32, name="f2_hi", tag="q_bf_then_f2", align_bytes=64)
+        nc.gpsimd.memset(f2_hi[:], 0.0)
 
         def score(dst, moving, moving_scale):
             nc.tensor.matmul_mx(
@@ -135,6 +134,9 @@ def tile_attend_audit_four_kernel(
             else:
                 nc.vector.tensor_copy(out=b[:, cols], in_=src)
 
+        f1 = sb.tile([P, POOL], F32, name="f1", tag="notes_codes1", align_bytes=64)
+        nc.gpsimd.memset(f1[:], 0.0)
+
         a = sb.tile([P, POOL], F32, name="a")
         col0 = 0
         for bank, width in zip((4, 5, 6, 7, 0), (256, 256, 256, 128, 128)):
@@ -154,38 +156,37 @@ def tile_attend_audit_four_kernel(
         nc.scalar.activation(a_got[:], a[:].indirect(half_list(token_list, 1)), COPY)
         nc.gpsimd.tensor_tensor(half(r, 1), a_got[:], half(b_got, 1), SUB)
 
-        for h in range(2):
+        for h, f2 in enumerate((f2_lo, f2_hi)):
             nc.vector.tensor_copy(f2[:].indirect(half_list(shelf_put_list, h)), half(r, h))
         nc.vector.tensor_copy(f1[:].indirect(user_put_list[:]), r[:])
 
-        split = POOL - GP_COLS
-        c0_tail = sb.tile([P, GP_COLS], F32, name="c0_tail")
-        score(banks[0][:, 0:GP_COLS], fp4_cols(users_codes, split, GP_COLS), users_plane[:, split:POOL])
-        nc.scalar.activation(c0_tail[:], banks[0][:, 0:GP_COLS], COPY)
-        score(banks[2][:], fp4_cols(users_codes, 0, BANK), users_plane[:, 0:BANK])
-        score(banks[3][:, 0 : split - BANK], fp4_cols(users_codes, BANK, split - BANK), users_plane[:, BANK:split])
-
-        d0 = sb.tile([P, POOL], F32, name="d0", tag="d0_then_cc")
-        for n in (1, 0):
+        d0 = sb.tile([P, POOL], F32, name="d0")
+        for n in range(2):
             cols = slice(n * BANK, (n + 1) * BANK)
             score(banks[n][:], fp8_cols(shelves_codes, n * BANK, BANK), shelves_plane[:, cols])
             nc.scalar.activation(d0[:, cols], banks[n][:], COPY)
 
+        split = POOL - GP_COLS
+        c0_tail = sb.tile([P, GP_COLS], F32, name="c0_tail")
+        score(banks[4][:, 0:GP_COLS], fp4_cols(users_codes, split, GP_COLS), users_plane[:, split:POOL])
+        nc.scalar.activation(c0_tail[:], banks[4][:, 0:GP_COLS], COPY)
+        score(banks[2][:], fp4_cols(users_codes, 0, BANK), users_plane[:, 0:BANK])
+        score(banks[3][:, 0 : split - BANK], fp4_cols(users_codes, BANK, split - BANK), users_plane[:, BANK:split])
+
+        d_part = sb.tile([P, POOL], F32, name="d_part", tag="d_part_then_cc")
+        nc.gpsimd.tensor_tensor(d_part[:], d0[:], f2_lo[:], SUB)
         dd = sb.tile([P, POOL], F32, name="dd")
-        nc.gpsimd.tensor_tensor(dd[:], d0[:], f2[:], SUB)
+        nc.gpsimd.tensor_tensor(dd[:], d_part[:], f2_hi[:], SUB)
         dd_got = sb.tile([P, SLOTS], F32, name="dd_got")
         for h in range(2):
             nc.scalar.activation(half(dd_got, h), dd[:].indirect(half_list(shelf_get_list, h)), COPY)
 
-        cc = sb.tile([P, POOL], F32, name="cc", tag="d0_then_cc")
+        cc = sb.tile([P, POOL], F32, name="cc", tag="d_part_then_cc")
         nc.gpsimd.tensor_tensor(cc[:, split:POOL], c0_tail[:], f1[:, split:POOL], ADD)
         nc.vector.tensor_tensor(cc[:, 0:BANK], banks[2][:], f1[:, 0:BANK], ADD)
         nc.vector.tensor_tensor(cc[:, BANK:split], banks[3][:, 0 : split - BANK], f1[:, BANK:split], ADD)
 
         y = sb.tile([P, SLOTS], F32, name="y")
-        nc.vector.tensor_tensor(half(y, 0), cc[:].indirect(half_list(user_get_list, 0)), half(dd_got, 0), SUB)
-        nc.sync.dma_start(out=out[:, 0:HALF], in_=half(y, 0))
-        cc_got = sb.tile([P, HALF], F32, name="cc_got")
-        nc.scalar.activation(cc_got[:], cc[:].indirect(half_list(user_get_list, 1)), COPY)
-        nc.vector.tensor_tensor(half(y, 1), cc_got[:], half(dd_got, 1), SUB)
-        nc.sync.dma_start(out=out[:, HALF:SLOTS], in_=half(y, 1))
+        for h in range(2):
+            nc.vector.tensor_tensor(half(y, h), cc[:].indirect(half_list(user_get_list, h)), half(dd_got, h), SUB)
+            nc.sync.dma_start(out=out[:, h * HALF : (h + 1) * HALF], in_=half(y, h))

from contextlib import ExitStack

import concourse.mybir as mybir

F32 = mybir.dt.float32
BF16 = mybir.dt.bfloat16
I32 = mybir.dt.int32
U32 = mybir.dt.uint32
U16 = mybir.dt.uint16
U8 = mybir.dt.uint8
FP8X4 = mybir.dt.float8_e4m3fn_x4
FP4X4 = mybir.dt.float4_e2m1fn_x4
ADD = mybir.AluOpType.add
SUB = mybir.AluOpType.subtract
COPY = mybir.ActivationFunctionType.Copy

P = 128
PACK = 4
POOL = 1024
SLOTS = 512
HALF = SLOTS // 2
BANK = 512
GP_COLS = 256
FLOPS = 2 * 512 * 128 * 4 * POOL


def tile_attend_audit_four_kernel(
    tc, query, keys_words, keys_scales, notes_words, notes_scales, users_words, users_scales,
    shelves_words, shelves_scales, offs, offs2, offs3, offs4, offs5, offs6, out,
):
    nc = tc.nc
    with ExitStack() as ctx:
        lists = ctx.enter_context(tc.tile_pool(name="lists", bufs=1))
        sb = ctx.enter_context(tc.tile_pool(name="sb", bufs=1))
        psum = ctx.enter_context(tc.psum_pool(name="psum", bufs=1))

        def scale_tile(name):
            plane = sb.tile([P, POOL], U8, name=name, align_bytes=64)
            nc.vector.memset(plane[:].bitcast(I32), 0)
            return plane

        def load_scale_rows(queue, plane, scales, quad):
            queue.dma_start(
                out=plane[32 * quad : 32 * quad + 4, :].bitcast(I32),
                in_=scales[0, 4 * quad : 4 * quad + 4, :].bitcast(I32),
            )

        def load_fp4(name, words):
            codes = sb.tile([P, 2 * POOL], U8, name=name, align_bytes=64)
            nc.sync.dma_start(out=codes[:].bitcast(I32), in_=words[0].bitcast(I32))
            return codes

        def load_fp8(name, words, col0, width):
            codes = sb.tile([P, width], U32, name=name, tag=name, align_bytes=64)
            src = words[0].rearrange("p n t -> p (n t)")[:, PACK * col0 : PACK * (col0 + width)]
            nc.sync.dma_start(out=codes[:].bitcast(I32), in_=src.bitcast(I32))
            return codes

        def load_list(name, src):
            tile = lists.tile([P, SLOTS // 16], U16, name=name)
            nc.sync.dma_start(tile[:], src)
            return tile

        notes_plane = scale_tile("notes_plane")
        keys_plane = scale_tile("keys_plane")
        shelves_plane = scale_tile("shelves_plane")
        users_plane = scale_tile("users_plane")
        f2_lo = sb.tile([P, POOL], F32, name="f2_lo")
        nc.vector.memset(f2_lo[:], 0.0)

        q_raw = sb.tile([P, PACK, P], F32, name="q_raw")
        nc.sync.dma_start(out=q_raw[:], in_=query.rearrange("(p j) w -> p j w", j=PACK))
        for quad in range(4):
            load_scale_rows(nc.sync if quad < 2 else nc.scalar, notes_plane, notes_scales, quad)
        notes_codes = [load_fp8("notes_codes%d" % h, notes_words, h * BANK, BANK) for h in range(2)]
        keys_codes = load_fp4("keys_codes", keys_words)
        for quad in range(4):
            load_scale_rows(nc.sync, keys_plane, keys_scales, quad)
        note_list = load_list("note_list", offs2)
        shelves_codes = load_fp8("shelves_codes", shelves_words, 0, POOL)
        token_list = load_list("token_list", offs)
        shelf_put_list = load_list("shelf_put_list", offs4)
        for quad in range(4):
            load_scale_rows(nc.sync, shelves_plane, shelves_scales, quad)
        users_codes = load_fp4("users_codes", users_words)
        for quad in range(4):
            load_scale_rows(nc.sync, users_plane, users_scales, quad)
        user_put_list = load_list("user_put_list", offs3)
        shelf_get_list = load_list("shelf_get_list", offs6)
        user_get_list = load_list("user_get_list", offs5)

        q_codes = sb.tile([P, P], U32, name="q_codes", align_bytes=64)
        q_plane = sb.tile([P, P], U8, name="q_plane", align_bytes=64)
        lo, hi = slice(0, P // 2), slice(P // 2, P)
        q_bf = sb.tile([P, P, PACK], BF16, name="q_bf", tag="q_bf_then_f2", align_bytes=64)
        nc.vector.tensor_copy(out=q_bf[:, lo, :], in_=q_raw[:, :, lo].rearrange("p j w -> p w j"))
        nc.scalar.activation(q_bf[:, hi, :], q_raw[:, :, hi].rearrange("p j w -> p w j"), COPY)
        for rows in (lo, hi):
            nc.vector.quantize_mx(
                out=q_codes[:, rows].bitcast(FP8X4), scales=q_plane[:, rows],
                in_=q_bf[:, rows, :].rearrange("p w j -> p (w j)"),
            )
        f2_hi = sb.tile([P, POOL], F32, name="f2_hi", tag="q_bf_then_f2", align_bytes=64)
        nc.gpsimd.memset(f2_hi[:], 0.0)

        def score(dst, moving, moving_scale):
            nc.tensor.matmul_mx(
                out=dst, lhsT=q_codes[:].bitcast(FP8X4), lhsT_scale=q_plane[:],
                rhs=moving, rhs_scale=moving_scale, start=True, stop=True,
            )

        def fp4_cols(codes, col0, width):
            return codes[:, 2 * col0 : 2 * (col0 + width)].bitcast(FP4X4)

        def fp8_cols(codes, col0, width):
            return codes[:, col0 : col0 + width].bitcast(FP8X4)

        banks = [psum.tile([P, BANK], F32, name="bank%d" % n) for n in range(8)]

        def half_list(tile, h):
            return tile[:, h * (HALF // 16) : (h + 1) * (HALF // 16)]

        def half(tile, h):
            return tile[:, h * HALF : (h + 1) * HALF]

        quarter = POOL // 4
        b = sb.tile([P, POOL], F32, name="b")
        for n in range(4):
            cols = slice(n * quarter, (n + 1) * quarter)
            src = banks[n][:, 0:quarter]
            score(src, fp8_cols(notes_codes[n // 2], (n % 2) * quarter, quarter), notes_plane[:, cols])
            if n % 2 == 0:
                nc.scalar.activation(b[:, cols], src, COPY)
            else:
                nc.vector.tensor_copy(out=b[:, cols], in_=src)

        f1 = sb.tile([P, POOL], F32, name="f1", tag="notes_codes1", align_bytes=64)
        nc.gpsimd.memset(f1[:], 0.0)

        a = sb.tile([P, POOL], F32, name="a")
        col0 = 0
        for bank, width in zip((4, 5, 6, 7, 0), (256, 256, 256, 128, 128)):
            cols = slice(col0, col0 + width)
            src = banks[bank][:, 0:width]
            score(src, fp4_cols(keys_codes, col0, width), keys_plane[:, cols])
            nc.vector.tensor_copy(out=a[:, cols], in_=src)
            col0 = col0 + width

        b_got = sb.tile([P, SLOTS], F32, name="b_got")
        for h in range(2):
            nc.scalar.activation(half(b_got, h), b[:].indirect(half_list(note_list, h)), COPY)

        r = sb.tile([P, SLOTS], F32, name="r")
        nc.vector.tensor_tensor(half(r, 0), a[:].indirect(half_list(token_list, 0)), half(b_got, 0), SUB)
        a_got = sb.tile([P, HALF], F32, name="a_got")
        nc.scalar.activation(a_got[:], a[:].indirect(half_list(token_list, 1)), COPY)
        nc.gpsimd.tensor_tensor(half(r, 1), a_got[:], half(b_got, 1), SUB)

        for h, f2 in enumerate((f2_lo, f2_hi)):
            nc.vector.tensor_copy(f2[:].indirect(half_list(shelf_put_list, h)), half(r, h))
        nc.vector.tensor_copy(f1[:].indirect(user_put_list[:]), r[:])

        d0 = sb.tile([P, POOL], F32, name="d0")
        for n in range(2):
            cols = slice(n * BANK, (n + 1) * BANK)
            score(banks[n][:], fp8_cols(shelves_codes, n * BANK, BANK), shelves_plane[:, cols])
            nc.scalar.activation(d0[:, cols], banks[n][:], COPY)

        split = POOL - GP_COLS
        c0_tail = sb.tile([P, GP_COLS], F32, name="c0_tail")
        score(banks[4][:, 0:GP_COLS], fp4_cols(users_codes, split, GP_COLS), users_plane[:, split:POOL])
        nc.scalar.activation(c0_tail[:], banks[4][:, 0:GP_COLS], COPY)
        score(banks[2][:], fp4_cols(users_codes, 0, BANK), users_plane[:, 0:BANK])
        score(banks[3][:, 0 : split - BANK], fp4_cols(users_codes, BANK, split - BANK), users_plane[:, BANK:split])

        d_part = sb.tile([P, POOL], F32, name="d_part", tag="d_part_then_cc")
        nc.gpsimd.tensor_tensor(d_part[:], d0[:], f2_lo[:], SUB)
        dd = sb.tile([P, POOL], F32, name="dd")
        nc.gpsimd.tensor_tensor(dd[:], d_part[:], f2_hi[:], SUB)
        dd_got = sb.tile([P, SLOTS], F32, name="dd_got")
        for h in range(2):
            nc.scalar.activation(half(dd_got, h), dd[:].indirect(half_list(shelf_get_list, h)), COPY)

        cc = sb.tile([P, POOL], F32, name="cc", tag="d_part_then_cc")
        nc.gpsimd.tensor_tensor(cc[:, split:POOL], c0_tail[:], f1[:, split:POOL], ADD)
        nc.vector.tensor_tensor(cc[:, 0:BANK], banks[2][:], f1[:, 0:BANK], ADD)
        nc.vector.tensor_tensor(cc[:, BANK:split], banks[3][:, 0 : split - BANK], f1[:, BANK:split], ADD)

        y = sb.tile([P, SLOTS], F32, name="y")
        for h in range(2):
            nc.vector.tensor_tensor(half(y, h), cc[:].indirect(half_list(user_get_list, h)), half(dd_got, h), SUB)
            nc.sync.dma_start(out=out[:, h * HALF : (h + 1) * HALF], in_=half(y, h))
